import numpy as np, ml_dtypes
CORES = [76,84,92,100,108,116,124]
N = 7
KB, QP, ROOT = 2, 32, 3
def setup_inputs(rng):
    return {"q": rng.standard_normal((N, 128, QP), dtype=np.float32).astype(ml_dtypes.bfloat16), "k": rng.standard_normal((N, 128, KB * 128), dtype=np.float32).astype(ml_dtypes.bfloat16), "v": rng.standard_normal((N, 128, KB * 128), dtype=np.float32).astype(ml_dtypes.bfloat16)}
def setup_inputs_big(rng):
    d = setup_inputs(rng)
    for k in ("q", "k", "v"): d[k] = (d[k].astype(np.float32) * 1024.0).astype(d[k].dtype)
    return d
def setup_inputs_small(rng):
    d = setup_inputs(rng)
    for k in ("q", "k", "v"): d[k] = (d[k].astype(np.float32) * (1 / 1024.0)).astype(d[k].dtype)
    return d
def setup_inputs_apart(rng):
    d = setup_inputs(rng)
    f = (10.0 ** rng.permutation(np.linspace(-1.5, 1.5, N))).astype(np.float32).reshape(N, 1, 1)
    for k in ("q", "k", "v"): d[k] = (d[k].astype(np.float32) * f).astype(d[k].dtype)
    return d
def reference(q, k, v):
    Q, K, V = q.astype(np.float64), k.astype(np.float64), v.astype(np.float64)
    o = np.zeros((128, QP))
    for j in range(N):
        for b in range(KB):
            o += V[j][:, 128 * b:128 * b + 128].T @ np.maximum(K[j][:, 128 * b:128 * b + 128].T @ Q[ROOT], 0.0)
    y = np.full((N, 128, QP), np.nan)
    y[ROOT] = o
    return {"y": y.astype(ml_dtypes.bfloat16 if q.dtype != np.float64 else np.float64)}

@@ -1,0 +1,185 @@
+from concourse.bass import DstId, RemoteDMATransfer
+from concourse.mybir import AluOpType
+
+P = 128
+QP = 32
+KB = 2
+NFWD = 2
+
+SCRATCH = {
+    "qs": ("sbuf", [P, QP], "bfloat16"),
+    "kv": ("sbuf", [P, 2 * KB * P], "bfloat16"),
+    "zero": ("sbuf", [P, KB * QP], "float32"),
+    "ss": ("sbuf", [P, KB * QP], "bfloat16"),
+    "ob": ("sbuf", [P, QP], "bfloat16"),
+    "land_n": ("sbuf", [P, 8 * QP], "bfloat16"),
+    "land_f": ("sbuf", [P, 8 * QP], "bfloat16"),
+    "acc": ("sbuf", [P, 8 * QP], "float32"),
+    "tree": ("sbuf", [P, 8 * QP], "float32"),
+    "ps_s": ("psum", [P, 512], "float32"),
+    "ps_o": ("psum", [P, 512], "float32"),
+}
+SEMAPHORES = ["qld", "kld", "vld", "qarr", "kvarr", "narr", "farr", "sent",
+              "zr", "m1", "rl", "m2", "cp", "va", "vt", "yr", "st"]
+
+
+def _bits(mask):
+    return [b for b in range(mask.bit_length()) if (mask >> b) & 1]
+
+
+def _part(mask, i, n):
+    b = _bits(mask)
+    w = len(b) // n
+    return sum(1 << e for e in b[i * w:(i + 1) * w])
+
+
+def _count(mask):
+    return len(_bits(mask))
+
+
+def _plan(T, topo):
+    cores = list(T.cores)
+    root = cores[T.root]
+    every = range(topo.CORES_PER_CHIP * topo.CHIPS)
+
+    def helpers(home, targets):
+        free = [x for x in every if topo.chip(x) == topo.chip(home) and x not in cores
+                and all(topo.may_write(x, t) for t in targets)]
+        return sorted(free, key=lambda x: (topo.die(x) != topo.die(home), x))
+
+    near = [c for c in cores if c != root and topo.may_write(root, c) and topo.may_write(c, root)]
+    far = [c for c in cores if c != root and c not in near]
+    worker = {c: helpers(c, [root])[0] for c in far}
+    fwd = helpers(root, list(worker.values()))[:NFWD] if far else []
+    serves = {h: [worker[c] for c in far[i::len(fwd)]] for i, h in enumerate(fwd)}
+    return root, near, far, worker, fwd, serves
+
+
+def _send(T, topo, dst, mask, sem, src, out):
+    rid, pid, _ = topo.addr(dst)
+    return RemoteDMATransfer(dst_ids=[DstId(rid=rid, pnc=pid)], dma_engine_mask=mask, remote_sem=sem, src=src, dst=out)
+
+
+def _attend(g, T, need_qk, need_v):
+    s = T.sem
+    g.vector.memset(T.zero[:], 0.0).then_inc(s.zr, 1)
+    for sem, n in need_qk:
+        g.tensor.wait_ge(sem, n)
+    for b in range(KB):
+        g.tensor.matmul(T.ps_s[:, b * QP:(b + 1) * QP], T.kv[:, b * P:(b + 1) * P], T.qs[:],
+                        start=True, stop=True).then_inc(s.m1, 1)
+    g.vector.wait_ge(s.zr, 1)
+    g.vector.wait_ge(s.m1, KB)
+    g.vector.tensor_tensor(T.ss[:], T.ps_s[:, 0:KB * QP], T.zero[:], AluOpType.max).then_inc(s.rl, 1)
+    g.tensor.wait_ge(s.rl, 1)
+    for sem, n in need_v:
+        g.tensor.wait_ge(sem, n)
+    for b in range(KB):
+        g.tensor.matmul(T.ps_o[:, 0:QP], T.kv[:, (KB + b) * P:(KB + b + 1) * P], T.ss[:, b * QP:(b + 1) * QP],
+                        start=(b == 0), stop=(b == KB - 1)).then_inc(s.m2, 1)
+
+
+def _return_partial(g, T, topo, core, root, out, sem):
+    s = T.sem
+    g.vector.wait_ge(s.m2, KB)
+    g.vector.tensor_copy(T.ob[:], T.ps_o[:, 0:QP]).then_inc(s.cp, 1)
+    g.wait_ge(s.cp, 1)
+    rid, pid, _ = topo.addr(root)
+    m = topo.mask(core, root)
+    g.remote_dma(out, T.ob[:], s[sem], s.sent, pid, rid, m)
+    g.wait_ge(s.sent, _count(m))
+
+
+def rank_program(g, core, T, topo):
+    s = T.sem
+    root, near, far, worker, fwd, serves = _plan(T, topo)
+    kcols, vcols = T.kv[:, 0:KB * P], T.kv[:, KB * P:2 * KB * P]
+
+    def q_mask_fwd(h):
+        return _part(topo.mask(root, h), fwd.index(h), len(fwd))
+
+    def q_mask_near(c):
+        return _part(topo.mask(root, c), near.index(c), len(near))
+
+    def q_mask_worker(h, w):
+        return _part(topo.mask(h, w), serves[h].index(w), len(serves[h]))
+
+    if core == root:
+        g.sync.dma_start(T.qs[:], T.q[:]).then_inc(s.qld, 16)
+        g.scalar.wait_ge(s.qld, 16)
+        g.scalar.dma_start(kcols, T.k[:]).then_inc(s.kld, 16)
+        g.scalar.dma_start(vcols, T.v[:]).then_inc(s.vld, 16)
+        g.wait_ge(s.qld, 16)
+        left = 0
+        for group, mask_of in ((fwd, q_mask_fwd), (near, q_mask_near)):
+            if group:
+                g.remote_dma_fused([_send(T, topo, d, mask_of(d), s.qarr, T.qs[:], T.qs[:]) for d in group],
+                                   local_sem=s.sent)
+                left += sum(_count(mask_of(d)) for d in group)
+        _attend(g, T, [(s.qld, 16), (s.kld, 16)], [(s.vld, 16)])
+        g.vector.wait_ge(s.m2, KB)
+        g.vector.wait_ge(s.narr, sum(_count(topo.mask(c, root)) for c in near))
+        have = T.ps_o[:, 0:QP]
+        for i in range(len(near)):
+            nxt = T.acc[:, i * QP:(i + 1) * QP]
+            g.vector.tensor_tensor(nxt, have, T.land_n[:, i * QP:(i + 1) * QP], AluOpType.add).then_inc(s.va, 1)
+            g.vector.wait_ge(s.va, i + 1)
+            have = nxt
+        g.vector.wait_ge(s.farr, sum(_count(topo.mask(worker[c], root)) for c in far))
+        buf, n, base, steps, odd, landed = T.land_f, len(far), 0, 0, [], True
+        while n > 1:
+            h = n // 2
+            if n % 2:
+                odd.append(buf[:, base + 2 * h * QP: base + n * QP])
+            out0 = 0 if landed else base + n * QP
+            g.vector.tensor_tensor(T.tree[:, out0:out0 + h * QP], buf[:, base:base + h * QP],
+                                   buf[:, base + h * QP:base + 2 * h * QP], AluOpType.add).then_inc(s.vt, 1)
+            steps += 1
+            g.vector.wait_ge(s.vt, steps)
+            buf, n, base, landed = T.tree, h, out0, False
+        terms = ([buf[:, base:base + QP]] if far else []) + odd
+        for i, t in enumerate(terms[:-1]):
+            nxt = T.acc[:, (len(near) + i) * QP:(len(near) + i + 1) * QP]
+            g.vector.tensor_tensor(nxt, have, t, AluOpType.add).then_inc(s.vt, 1)
+            steps += 1
+            g.vector.wait_ge(s.vt, steps)
+            have = nxt
+        if terms:
+            g.vector.tensor_tensor(T.ob[:], have, terms[-1], AluOpType.add).then_inc(s.yr, 1)
+        else:
+            g.vector.tensor_copy(T.ob[:], have).then_inc(s.yr, 1)
+        g.sync.wait_ge(s.yr, 1)
+        g.sync.dma_start(T.y[:], T.ob[:]).then_inc(s.st, 16)
+        g.wait_ge(s.sent, left)
+        g.wait_ge(s.st, 16)
+
+    elif core in near:
+        g.sync.dma_start(kcols, T.k[:]).then_inc(s.kld, 16)
+        g.scalar.dma_start(vcols, T.v[:]).then_inc(s.vld, 16)
+        _attend(g, T, [(s.kld, 16), (s.qarr, _count(q_mask_near(core)))], [(s.vld, 16)])
+        i = near.index(core)
+        _return_partial(g, T, topo, core, root, T.land_n[:, i * QP:(i + 1) * QP], "narr")
+
+    elif core in far:
+        w = worker[core]
+        g.sync.dma_start(kcols, T.k[:]).then_inc(s.kld, 16)
+        g.scalar.dma_start(vcols, T.v[:]).then_inc(s.vld, 16)
+        g.wait_ge(s.kld, 16)
+        g.wait_ge(s.vld, 16)
+        rid, pid, _ = topo.addr(w)
+        m = topo.mask(core, w)
+        g.remote_dma(T.kv[:], T.kv[:], s.kvarr, s.sent, pid, rid, m)
+        g.wait_ge(s.sent, _count(m))
+
+    elif core in fwd:
+        g.wait_ge(s.qarr, _count(q_mask_fwd(core)))
+        g.remote_dma_fused([_send(T, topo, w, q_mask_worker(core, w), s.qarr, T.qs[:], T.qs[:]) for w in serves[core]],
+                           local_sem=s.sent)
+        g.wait_ge(s.sent, sum(_count(q_mask_worker(core, w)) for w in serves[core]))
+
+    elif core in worker.values():
+        c = [r for r in far if worker[r] == core][0]
+        h = [f for f in fwd if core in serves[f]][0]
+        _attend(g, T, [(s.kvarr, _count(topo.mask(c, core))), (s.qarr, _count(q_mask_worker(h, core)))], [])
+        i = far.index(c)
+        _return_partial(g, T, topo, core, root, T.land_f[:, i * QP:(i + 1) * QP], "farr")

@@ -4,23 +4,25 @@ from concourse.mybir import AluOpType
 P = 128
 QP = 32
 KB = 2
-NFWD = 2
+NF = 4
+W = 2 * KB * P
 
 SCRATCH = {
     "qs": ("sbuf", [P, QP], "bfloat16"),
-    "kv": ("sbuf", [P, 2 * KB * P], "bfloat16"),
-    "zero": ("sbuf", [P, KB * QP], "float32"),
+    "kv": ("sbuf", [P, W], "bfloat16"),
+    "fkv": ("sbuf", [P, NF * W], "bfloat16"),
+    "zero": ("sbuf", [P, NF * KB * QP], "float32"),
     "ss": ("sbuf", [P, KB * QP], "bfloat16"),
+    "sf": ("sbuf", [P, NF * KB * QP], "bfloat16"),
     "ob": ("sbuf", [P, QP], "bfloat16"),
     "land_n": ("sbuf", [P, 8 * QP], "bfloat16"),
-    "land_f": ("sbuf", [P, 8 * QP], "bfloat16"),
     "acc": ("sbuf", [P, 8 * QP], "float32"),
-    "tree": ("sbuf", [P, 8 * QP], "float32"),
     "ps_s": ("psum", [P, 512], "float32"),
+    "ps_f": ("psum", [P, 512], "float32"),
     "ps_o": ("psum", [P, 512], "float32"),
 }
-SEMAPHORES = ["qld", "kld", "vld", "qarr", "kvarr", "narr", "farr", "sent",
-              "zr", "m1", "rl", "m2", "cp", "va", "vt", "yr", "st"]
+SEMAPHORES = ["qld", "kld", "vld", "qarr", "karr", "varr", "narr", "sent",
+              "zr", "m1", "rl", "mf", "rf", "m2", "cp", "va", "yr", "st"]
 
 
 def _bits(mask):
@@ -41,26 +43,23 @@ def _plan(T, topo):
     cores = list(T.cores)
     root = cores[T.root]
     every = range(topo.CORES_PER_CHIP * topo.CHIPS)
-
-    def helpers(home, targets):
-        free = [x for x in every if topo.chip(x) == topo.chip(home) and x not in cores
-                and all(topo.may_write(x, t) for t in targets)]
-        return sorted(free, key=lambda x: (topo.die(x) != topo.die(home), x))
-
     near = [c for c in cores if c != root and topo.may_write(root, c) and topo.may_write(c, root)]
     far = [c for c in cores if c != root and c not in near]
-    worker = {c: helpers(c, [root])[0] for c in far}
-    fwd = helpers(root, list(worker.values()))[:NFWD] if far else []
-    serves = {h: [worker[c] for c in far[i::len(fwd)]] for i, h in enumerate(fwd)}
-    return root, near, far, worker, fwd, serves
+    carriers = {}
+    for c in far:
+        free = [x for x in every if topo.chip(x) == topo.chip(c) and x not in cores and topo.may_write(x, root)]
+        dies = sorted({topo.die(x) for x in free}, key=lambda d: d != topo.die(c))
+        first = [[x for x in free if topo.die(x) == d] for d in dies]
+        carriers[c] = [first[b % len(first)][b // len(first)] for b in range(KB)]
+    return root, near, far, carriers
 
 
-def _send(T, topo, dst, mask, sem, src, out):
+def _send(topo, dst, mask, sem, src, out):
     rid, pid, _ = topo.addr(dst)
     return RemoteDMATransfer(dst_ids=[DstId(rid=rid, pnc=pid)], dma_engine_mask=mask, remote_sem=sem, src=src, dst=out)
 
 
-def _attend(g, T, need_qk, need_v):
+def _attend(g, T, need_qk, need_v, close):
     s = T.sem
     g.vector.memset(T.zero[:], 0.0).then_inc(s.zr, 1)
     for sem, n in need_qk:
@@ -70,39 +69,29 @@ def _attend(g, T, need_qk, need_v):
                         start=True, stop=True).then_inc(s.m1, 1)
     g.vector.wait_ge(s.zr, 1)
     g.vector.wait_ge(s.m1, KB)
-    g.vector.tensor_tensor(T.ss[:], T.ps_s[:, 0:KB * QP], T.zero[:], AluOpType.max).then_inc(s.rl, 1)
+    g.vector.tensor_tensor(T.ss[:], T.ps_s[:, 0:KB * QP], T.zero[:, 0:KB * QP], AluOpType.max).then_inc(s.rl, 1)
     g.tensor.wait_ge(s.rl, 1)
     for sem, n in need_v:
         g.tensor.wait_ge(sem, n)
     for b in range(KB):
         g.tensor.matmul(T.ps_o[:, 0:QP], T.kv[:, (KB + b) * P:(KB + b + 1) * P], T.ss[:, b * QP:(b + 1) * QP],
-                        start=(b == 0), stop=(b == KB - 1)).then_inc(s.m2, 1)
-
-
-def _return_partial(g, T, topo, core, root, out, sem):
-    s = T.sem
-    g.vector.wait_ge(s.m2, KB)
-    g.vector.tensor_copy(T.ob[:], T.ps_o[:, 0:QP]).then_inc(s.cp, 1)
-    g.wait_ge(s.cp, 1)
-    rid, pid, _ = topo.addr(root)
-    m = topo.mask(core, root)
-    g.remote_dma(out, T.ob[:], s[sem], s.sent, pid, rid, m)
-    g.wait_ge(s.sent, _count(m))
+                        start=(b == 0), stop=(close and b == KB - 1)).then_inc(s.m2, 1)
 
 
 def rank_program(g, core, T, topo):
     s = T.sem
-    root, near, far, worker, fwd, serves = _plan(T, topo)
+    root, near, far, carriers = _plan(T, topo)
     kcols, vcols = T.kv[:, 0:KB * P], T.kv[:, KB * P:2 * KB * P]
+    nf = len(far)
 
-    def q_mask_fwd(h):
-        return _part(topo.mask(root, h), fwd.index(h), len(fwd))
+    def blk(t, base, i):
+        return t[:, base + i * P:base + (i + 1) * P]
 
     def q_mask_near(c):
         return _part(topo.mask(root, c), near.index(c), len(near))
 
-    def q_mask_worker(h, w):
-        return _part(topo.mask(h, w), serves[h].index(w), len(serves[h]))
+    def feed_mask(c, b):
+        return _part(topo.mask(c, carriers[c][b]), b, KB)
 
     if core == root:
         g.sync.dma_start(T.qs[:], T.q[:]).then_inc(s.qld, 16)
@@ -110,76 +99,65 @@ def rank_program(g, core, T, topo):
         g.scalar.dma_start(kcols, T.k[:]).then_inc(s.kld, 16)
         g.scalar.dma_start(vcols, T.v[:]).then_inc(s.vld, 16)
         g.wait_ge(s.qld, 16)
-        left = 0
-        for group, mask_of in ((fwd, q_mask_fwd), (near, q_mask_near)):
-            if group:
-                g.remote_dma_fused([_send(T, topo, d, mask_of(d), s.qarr, T.qs[:], T.qs[:]) for d in group],
-                                   local_sem=s.sent)
-                left += sum(_count(mask_of(d)) for d in group)
-        _attend(g, T, [(s.qld, 16), (s.kld, 16)], [(s.vld, 16)])
-        g.vector.wait_ge(s.m2, KB)
+        g.remote_dma_fused([_send(topo, c, q_mask_near(c), s.qarr, T.qs[:], T.qs[:]) for c in near], local_sem=s.sent)
+        _attend(g, T, [(s.qld, 16), (s.kld, 16)], [(s.vld, 16)], close=(nf == 0))
+        landed = sum(_count(topo.mask(x, root)) for c in far for x in carriers[c])
+        g.tensor.wait_ge(s.karr, landed)
+        for i in range(nf * KB):
+            g.tensor.matmul(T.ps_f[:, i * QP:(i + 1) * QP], blk(T.fkv, (i // KB) * W, i % KB), T.qs[:],
+                            start=True, stop=True).then_inc(s.mf, 1)
+        g.vector.wait_ge(s.mf, nf * KB)
+        g.vector.tensor_tensor(T.sf[:, 0:nf * KB * QP], T.ps_f[:, 0:nf * KB * QP], T.zero[:, 0:nf * KB * QP],
+                               AluOpType.max).then_inc(s.rf, 1)
+        g.tensor.wait_ge(s.rf, 1)
+        g.tensor.wait_ge(s.varr, landed)
+        for i in range(nf * KB):
+            g.tensor.matmul(T.ps_o[:, 0:QP], blk(T.fkv, (i // KB) * W, KB + i % KB), T.sf[:, i * QP:(i + 1) * QP],
+                            start=False, stop=(i == nf * KB - 1)).then_inc(s.m2, 1)
         g.vector.wait_ge(s.narr, sum(_count(topo.mask(c, root)) for c in near))
-        have = T.ps_o[:, 0:QP]
-        for i in range(len(near)):
+        have = T.land_n[:, 0:QP]
+        for i in range(1, len(near)):
             nxt = T.acc[:, i * QP:(i + 1) * QP]
             g.vector.tensor_tensor(nxt, have, T.land_n[:, i * QP:(i + 1) * QP], AluOpType.add).then_inc(s.va, 1)
-            g.vector.wait_ge(s.va, i + 1)
+            g.vector.wait_ge(s.va, i)
             have = nxt
-        g.vector.wait_ge(s.farr, sum(_count(topo.mask(worker[c], root)) for c in far))
-        buf, n, base, steps, odd, landed = T.land_f, len(far), 0, 0, [], True
-        while n > 1:
-            h = n // 2
-            if n % 2:
-                odd.append(buf[:, base + 2 * h * QP: base + n * QP])
-            out0 = 0 if landed else base + n * QP
-            g.vector.tensor_tensor(T.tree[:, out0:out0 + h * QP], buf[:, base:base + h * QP],
-                                   buf[:, base + h * QP:base + 2 * h * QP], AluOpType.add).then_inc(s.vt, 1)
-            steps += 1
-            g.vector.wait_ge(s.vt, steps)
-            buf, n, base, landed = T.tree, h, out0, False
-        terms = ([buf[:, base:base + QP]] if far else []) + odd
-        for i, t in enumerate(terms[:-1]):
-            nxt = T.acc[:, (len(near) + i) * QP:(len(near) + i + 1) * QP]
-            g.vector.tensor_tensor(nxt, have, t, AluOpType.add).then_inc(s.vt, 1)
-            steps += 1
-            g.vector.wait_ge(s.vt, steps)
-            have = nxt
-        if terms:
-            g.vector.tensor_tensor(T.ob[:], have, terms[-1], AluOpType.add).then_inc(s.yr, 1)
-        else:
-            g.vector.tensor_copy(T.ob[:], have).then_inc(s.yr, 1)
+        g.vector.wait_ge(s.m2, KB + nf * KB)
+        g.vector.tensor_tensor(T.ob[:], T.ps_o[:, 0:QP], have, AluOpType.add).then_inc(s.yr, 1)
         g.sync.wait_ge(s.yr, 1)
         g.sync.dma_start(T.y[:], T.ob[:]).then_inc(s.st, 16)
-        g.wait_ge(s.sent, left)
+        g.wait_ge(s.sent, sum(_count(q_mask_near(c)) for c in near))
         g.wait_ge(s.st, 16)
 
     elif core in near:
         g.sync.dma_start(kcols, T.k[:]).then_inc(s.kld, 16)
         g.scalar.dma_start(vcols, T.v[:]).then_inc(s.vld, 16)
-        _attend(g, T, [(s.kld, 16), (s.qarr, _count(q_mask_near(core)))], [(s.vld, 16)])
+        _attend(g, T, [(s.kld, 16), (s.qarr, _count(q_mask_near(core)))], [(s.vld, 16)], close=True)
+        g.vector.wait_ge(s.m2, KB)
+        g.vector.tensor_copy(T.ob[:], T.ps_o[:, 0:QP]).then_inc(s.cp, 1)
+        g.wait_ge(s.cp, 1)
+        rid, pid, _ = topo.addr(root)
+        m = topo.mask(core, root)
         i = near.index(core)
-        _return_partial(g, T, topo, core, root, T.land_n[:, i * QP:(i + 1) * QP], "narr")
-
-    elif core in far:
-        w = worker[core]
-        g.sync.dma_start(kcols, T.k[:]).then_inc(s.kld, 16)
-        g.scalar.dma_start(vcols, T.v[:]).then_inc(s.vld, 16)
-        g.wait_ge(s.kld, 16)
-        g.wait_ge(s.vld, 16)
-        rid, pid, _ = topo.addr(w)
-        m = topo.mask(core, w)
-        g.remote_dma(T.kv[:], T.kv[:], s.kvarr, s.sent, pid, rid, m)
+        g.remote_dma(T.land_n[:, i * QP:(i + 1) * QP], T.ob[:], s.narr, s.sent, pid, rid, m)
         g.wait_ge(s.sent, _count(m))
 
-    elif core in fwd:
-        g.wait_ge(s.qarr, _count(q_mask_fwd(core)))
-        g.remote_dma_fused([_send(T, topo, w, q_mask_worker(core, w), s.qarr, T.qs[:], T.qs[:]) for w in serves[core]],
-                           local_sem=s.sent)
-        g.wait_ge(s.sent, sum(_count(q_mask_worker(core, w)) for w in serves[core]))
+    elif core in far:
+        g.sync.dma_start(kcols, T.k[:]).then_inc(s.kld, 16)
+        g.sync.dma_start(vcols, T.v[:]).then_inc(s.vld, 16)
+        for loaded, sem, first in ((s.kld, s.karr, 0), (s.vld, s.varr, KB)):
+            g.wait_ge(loaded, 16)
+            g.remote_dma_fused([_send(topo, carriers[core][b], feed_mask(core, b), sem,
+                                      blk(T.kv, 0, first + b), blk(T.kv, 0, first + b)) for b in range(KB)],
+                               local_sem=s.sent)
+        g.wait_ge(s.sent, 2 * sum(_count(feed_mask(core, b)) for b in range(KB)))
 
-    elif core in worker.values():
-        c = [r for r in far if worker[r] == core][0]
-        h = [f for f in fwd if core in serves[f]][0]
-        _attend(g, T, [(s.kvarr, _count(topo.mask(c, core))), (s.qarr, _count(q_mask_worker(h, core)))], [])
-        i = far.index(c)
-        _return_partial(g, T, topo, core, root, T.land_f[:, i * QP:(i + 1) * QP], "farr")
+    else:
+        for j, c in enumerate(far):
+            if core in carriers[c]:
+                b = carriers[c].index(core)
+                rid, pid, _ = topo.addr(root)
+                m = topo.mask(core, root)
+                for sem, first in ((s.karr, 0), (s.varr, KB)):
+                    g.wait_ge(sem, _count(feed_mask(c, b)))
+                    g.remote_dma(blk(T.fkv, j * W, first + b), blk(T.kv, 0, first + b), sem, s.sent, pid, rid, m)
+                g.wait_ge(s.sent, 2 * _count(m))

@@ -5,24 +5,32 @@ P = 128
 QP = 32
 KB = 2
 NF = 4
-W = 2 * KB * P
+NN = 2
+NC = 4
+KW = KB * P
+W = 2 * KW
+H = 8
 
 SCRATCH = {
     "qs": ("sbuf", [P, QP], "bfloat16"),
     "kv": ("sbuf", [P, W], "bfloat16"),
+    "hd": ("dram", [NC, P, H], "bfloat16"),
     "fkv": ("sbuf", [P, NF * W], "bfloat16"),
-    "zero": ("sbuf", [P, NF * KB * QP], "float32"),
+    "nv": ("sbuf", [P, NN * KW], "bfloat16"),
+    "ns": ("sbuf", [P, NN * KB * QP], "bfloat16"),
+    "zero": ("sbuf", [P, KB * QP], "float32"),
     "ss": ("sbuf", [P, KB * QP], "bfloat16"),
     "sf": ("sbuf", [P, NF * KB * QP], "bfloat16"),
     "ob": ("sbuf", [P, QP], "bfloat16"),
-    "land_n": ("sbuf", [P, 8 * QP], "bfloat16"),
-    "acc": ("sbuf", [P, 8 * QP], "float32"),
     "ps_s": ("psum", [P, 512], "float32"),
-    "ps_f": ("psum", [P, 512], "float32"),
     "ps_o": ("psum", [P, 512], "float32"),
 }
-SEMAPHORES = ["qld", "kld", "vld", "qarr", "karr", "varr", "narr", "sent",
-              "zr", "m1", "rl", "mf", "rf", "m2", "cp", "va", "yr", "st"]
+for _j in range(NF):
+    SCRATCH["ps_f%d" % _j] = ("psum", [P, 512], "float32")
+SEMAPHORES = ["qld", "kld", "vld", "hld", "qarr", "harr", "karr", "varr", "narr", "nvarr", "sent",
+              "zr", "m1", "rl", "m2", "yr", "st"]
+SEMAPHORES += [n % j for j in range(NF) for n in ("ka%d", "mf%d", "rf%d")]
+SEMAPHORES += ["vb%d" % i for i in range(NF * KB)]
 
 
 def _bits(mask):
@@ -45,12 +53,19 @@ def _plan(T, topo):
     every = range(topo.CORES_PER_CHIP * topo.CHIPS)
     near = [c for c in cores if c != root and topo.may_write(root, c) and topo.may_write(c, root)]
     far = [c for c in cores if c != root and c not in near]
-    carriers = {}
-    for c in far:
+
+    def owners(c):
         free = [x for x in every if topo.chip(x) == topo.chip(c) and x not in cores and topo.may_write(x, root)]
         dies = sorted({topo.die(x) for x in free}, key=lambda d: d != topo.die(c))
         first = [[x for x in free if topo.die(x) == d] for d in dies]
-        carriers[c] = [first[b % len(first)][b // len(first)] for b in range(KB)]
+        return [first[b % len(first)][b // len(first)] for b in range(len(free))][0:NC]
+
+    carriers = {c: owners(c) for c in far}
+    beside = [c for c in far if topo.mates(topo.chip(c), topo.chip(root))]
+    beyond = [c for c in far if c not in beside and all(topo.may_write(c, x) for b in beside for x in owners(b))]
+    if beside and beyond:
+        pool = owners(beside[0])
+        carriers[beside[0]], carriers[beyond[0]] = pool[0:len(pool) // 2], pool[len(pool) // 2:]
     return root, near, far, carriers
 
 
@@ -59,39 +74,40 @@ def _send(topo, dst, mask, sem, src, out):
     return RemoteDMATransfer(dst_ids=[DstId(rid=rid, pnc=pid)], dma_engine_mask=mask, remote_sem=sem, src=src, dst=out)
 
 
-def _attend(g, T, need_qk, need_v, close):
+def _scores(g, T, need):
     s = T.sem
     g.vector.memset(T.zero[:], 0.0).then_inc(s.zr, 1)
-    for sem, n in need_qk:
+    for sem, n in need:
         g.tensor.wait_ge(sem, n)
     for b in range(KB):
         g.tensor.matmul(T.ps_s[:, b * QP:(b + 1) * QP], T.kv[:, b * P:(b + 1) * P], T.qs[:],
                         start=True, stop=True).then_inc(s.m1, 1)
     g.vector.wait_ge(s.zr, 1)
     g.vector.wait_ge(s.m1, KB)
-    g.vector.tensor_tensor(T.ss[:], T.ps_s[:, 0:KB * QP], T.zero[:, 0:KB * QP], AluOpType.max).then_inc(s.rl, 1)
-    g.tensor.wait_ge(s.rl, 1)
-    for sem, n in need_v:
-        g.tensor.wait_ge(sem, n)
-    for b in range(KB):
-        g.tensor.matmul(T.ps_o[:, 0:QP], T.kv[:, (KB + b) * P:(KB + b + 1) * P], T.ss[:, b * QP:(b + 1) * QP],
-                        start=(b == 0), stop=(close and b == KB - 1)).then_inc(s.m2, 1)
+    g.vector.tensor_tensor(T.ss[:], T.ps_s[:, 0:KB * QP], T.zero[:], AluOpType.max).then_inc(s.rl, 1)
 
 
 def rank_program(g, core, T, topo):
     s = T.sem
     root, near, far, carriers = _plan(T, topo)
-    kcols, vcols = T.kv[:, 0:KB * P], T.kv[:, KB * P:2 * KB * P]
-    nf = len(far)
+    kcols, vcols = T.kv[:, 0:KW], T.kv[:, KW:W]
+    nf, nn = len(far), len(near)
 
-    def blk(t, base, i):
-        return t[:, base + i * P:base + (i + 1) * P]
+    def cols(t, a, n):
+        return t[:, a:a + n]
 
-    def q_mask_near(c):
-        return _part(topo.mask(root, c), near.index(c), len(near))
+    def q_mask(c):
+        return _part(topo.mask(root, c), near.index(c), nn)
 
-    def feed_mask(c, b):
-        return _part(topo.mask(c, carriers[c][b]), b, KB)
+    def head_mask(c, i):
+        m = topo.mask(c, carriers[c][i])
+        return _part(m, i, _count(m))
+
+    def feed_mask(c, i):
+        return _part(topo.mask(c, carriers[c][i]), i, len(carriers[c]))
+
+    def c_mask(x):
+        return topo.mask(x, root)
 
     if core == root:
         g.sync.dma_start(T.qs[:], T.q[:]).then_inc(s.qld, 16)
@@ -99,65 +115,87 @@ def rank_program(g, core, T, topo):
         g.scalar.dma_start(kcols, T.k[:]).then_inc(s.kld, 16)
         g.scalar.dma_start(vcols, T.v[:]).then_inc(s.vld, 16)
         g.wait_ge(s.qld, 16)
-        g.remote_dma_fused([_send(topo, c, q_mask_near(c), s.qarr, T.qs[:], T.qs[:]) for c in near], local_sem=s.sent)
-        _attend(g, T, [(s.qld, 16), (s.kld, 16)], [(s.vld, 16)], close=(nf == 0))
-        landed = sum(_count(topo.mask(x, root)) for c in far for x in carriers[c])
-        g.tensor.wait_ge(s.karr, landed)
-        for i in range(nf * KB):
-            g.tensor.matmul(T.ps_f[:, i * QP:(i + 1) * QP], blk(T.fkv, (i // KB) * W, i % KB), T.qs[:],
-                            start=True, stop=True).then_inc(s.mf, 1)
-        g.vector.wait_ge(s.mf, nf * KB)
-        g.vector.tensor_tensor(T.sf[:, 0:nf * KB * QP], T.ps_f[:, 0:nf * KB * QP], T.zero[:, 0:nf * KB * QP],
-                               AluOpType.max).then_inc(s.rf, 1)
-        g.tensor.wait_ge(s.rf, 1)
-        g.tensor.wait_ge(s.varr, landed)
-        for i in range(nf * KB):
-            g.tensor.matmul(T.ps_o[:, 0:QP], blk(T.fkv, (i // KB) * W, KB + i % KB), T.sf[:, i * QP:(i + 1) * QP],
-                            start=False, stop=(i == nf * KB - 1)).then_inc(s.m2, 1)
-        g.vector.wait_ge(s.narr, sum(_count(topo.mask(c, root)) for c in near))
-        have = T.land_n[:, 0:QP]
-        for i in range(1, len(near)):
-            nxt = T.acc[:, i * QP:(i + 1) * QP]
-            g.vector.tensor_tensor(nxt, have, T.land_n[:, i * QP:(i + 1) * QP], AluOpType.add).then_inc(s.va, 1)
-            g.vector.wait_ge(s.va, i)
-            have = nxt
-        g.vector.wait_ge(s.m2, KB + nf * KB)
-        g.vector.tensor_tensor(T.ob[:], T.ps_o[:, 0:QP], have, AluOpType.add).then_inc(s.yr, 1)
+        g.remote_dma_fused([_send(topo, c, q_mask(c), s.qarr, T.qs[:], T.qs[:]) for c in near], local_sem=s.sent)
+        _scores(g, T, [(s.qld, 16), (s.kld, 16)])
+        g.tensor.wait_ge(s.rl, 1)
+        g.tensor.wait_ge(s.vld, 16)
+        for b in range(KB):
+            g.tensor.matmul(T.ps_o[:, 0:QP], cols(T.kv, KW + b * P, P), cols(T.ss, b * QP, QP),
+                            start=(b == 0), stop=False).then_inc(s.m2, 1)
+        back = sum(_count(topo.mask(c, root)) for c in near)
+        g.tensor.wait_ge(s.nvarr, back)
+        g.tensor.wait_ge(s.narr, back)
+        for i in range(nn * KB):
+            g.tensor.matmul(T.ps_o[:, 0:QP], cols(T.nv, i * P, P), cols(T.ns, i * QP, QP),
+                            start=False, stop=False).then_inc(s.m2, 1)
+        order = sorted(range(nf), key=lambda j: (topo.chip(carriers[far[j]][0]) != topo.chip(far[j]),
+                                                 -len(carriers[far[j]])))
+        for j in order:
+            g.tensor.wait_ge(s["ka%d" % j], 2 * sum(_count(c_mask(x)) for x in carriers[far[j]]))
+            pf = T["ps_f%d" % j]
+            for b in range(KB):
+                g.tensor.matmul(cols(pf, b * QP, QP), cols(T.fkv, j * W + b * P, P), T.qs[:],
+                                start=True, stop=True).then_inc(s["mf%d" % j], 1)
+            g.vector.wait_ge(s["mf%d" % j], KB)
+            g.vector.tensor_tensor(cols(T.sf, j * KB * QP, KB * QP), pf[:, 0:KB * QP], T.zero[:],
+                                   AluOpType.max).then_inc(s["rf%d" % j], 1)
+        for j in order:
+            g.tensor.wait_ge(s["rf%d" % j], 1)
+            per = len(carriers[far[j]]) // KB
+            for b in range(KB):
+                g.tensor.wait_ge(s["vb%d" % (j * KB + b)],
+                                 sum(_count(c_mask(x)) for x in carriers[far[j]][b * per:(b + 1) * per]))
+                g.tensor.matmul(T.ps_o[:, 0:QP], cols(T.fkv, j * W + KW + b * P, P), cols(T.sf, (j * KB + b) * QP, QP),
+                                start=False, stop=(j == order[-1] and b == KB - 1)).then_inc(s.m2, 1)
+        g.vector.wait_ge(s.m2, (1 + nn + nf) * KB)
+        g.vector.tensor_copy(T.ob[:], T.ps_o[:, 0:QP]).then_inc(s.yr, 1)
         g.sync.wait_ge(s.yr, 1)
         g.sync.dma_start(T.y[:], T.ob[:]).then_inc(s.st, 16)
-        g.wait_ge(s.sent, sum(_count(q_mask_near(c)) for c in near))
+        g.wait_ge(s.sent, sum(_count(q_mask(c)) for c in near))
         g.wait_ge(s.st, 16)
 
     elif core in near:
-        g.sync.dma_start(kcols, T.k[:]).then_inc(s.kld, 16)
-        g.scalar.dma_start(vcols, T.v[:]).then_inc(s.vld, 16)
-        _attend(g, T, [(s.kld, 16), (s.qarr, _count(q_mask_near(core)))], [(s.vld, 16)], close=True)
-        g.vector.wait_ge(s.m2, KB)
-        g.vector.tensor_copy(T.ob[:], T.ps_o[:, 0:QP]).then_inc(s.cp, 1)
-        g.wait_ge(s.cp, 1)
+        i = near.index(core)
         rid, pid, _ = topo.addr(root)
         m = topo.mask(core, root)
-        i = near.index(core)
-        g.remote_dma(T.land_n[:, i * QP:(i + 1) * QP], T.ob[:], s.narr, s.sent, pid, rid, m)
-        g.wait_ge(s.sent, _count(m))
+        g.sync.dma_start(vcols, T.v[:]).then_inc(s.vld, 16)
+        g.scalar.dma_start(kcols, T.k[:]).then_inc(s.kld, 16)
+        g.wait_ge(s.vld, 16)
+        g.remote_dma(cols(T.nv, i * KW, KW), vcols, s.nvarr, s.sent, pid, rid, m)
+        _scores(g, T, [(s.kld, 16), (s.qarr, _count(q_mask(core)))])
+        g.wait_ge(s.rl, 1)
+        g.remote_dma(cols(T.ns, i * KB * QP, KB * QP), T.ss[:], s.narr, s.sent, pid, rid, m)
+        g.wait_ge(s.sent, 2 * _count(m))
 
     elif core in far:
+        mine = carriers[core]
+        nc = len(mine)
+        cw = KW // nc
+        for i in range(nc):
+            (g.sync, g.scalar)[i % 2].dma_start(T.hd[i], cols(T.k, i * cw, H)).then_inc(s.hld, 16)
         g.sync.dma_start(kcols, T.k[:]).then_inc(s.kld, 16)
-        g.sync.dma_start(vcols, T.v[:]).then_inc(s.vld, 16)
-        for loaded, sem, first in ((s.kld, s.karr, 0), (s.vld, s.varr, KB)):
+        g.scalar.dma_start(vcols, T.v[:]).then_inc(s.vld, 16)
+        g.wait_ge(s.hld, 16 * nc)
+        g.remote_dma_fused([_send(topo, mine[i], head_mask(core, i), s.harr, T.hd[i], T.hd[i]) for i in range(nc)],
+                           local_sem=s.sent)
+        for loaded, sem, a, n in ((s.kld, s.karr, H, cw - H), (s.vld, s.varr, KW, cw)):
             g.wait_ge(loaded, 16)
-            g.remote_dma_fused([_send(topo, carriers[core][b], feed_mask(core, b), sem,
-                                      blk(T.kv, 0, first + b), blk(T.kv, 0, first + b)) for b in range(KB)],
+            g.remote_dma_fused([_send(topo, mine[i], feed_mask(core, i), sem,
+                                      cols(T.kv, a + i * cw, n), cols(T.kv, a + i * cw, n)) for i in range(nc)],
                                local_sem=s.sent)
-        g.wait_ge(s.sent, 2 * sum(_count(feed_mask(core, b)) for b in range(KB)))
+        g.wait_ge(s.sent, sum(_count(head_mask(core, i)) + 2 * _count(feed_mask(core, i)) for i in range(nc)))
 
     else:
         for j, c in enumerate(far):
             if core in carriers[c]:
-                b = carriers[c].index(core)
+                i = carriers[c].index(core)
+                cw = KW // len(carriers[c])
                 rid, pid, _ = topo.addr(root)
-                m = topo.mask(core, root)
-                for sem, first in ((s.karr, 0), (s.varr, KB)):
-                    g.wait_ge(sem, _count(feed_mask(c, b)))
-                    g.remote_dma(blk(T.fkv, j * W, first + b), blk(T.kv, 0, first + b), sem, s.sent, pid, rid, m)
-                g.wait_ge(s.sent, 2 * _count(m))
+                m = c_mask(core)
+                k_here, v_here = s["ka%d" % j], s["vb%d" % (j * KB + i * cw // P)]
+                g.wait_ge(s.harr, _count(head_mask(c, i)))
+                g.remote_dma(cols(T.fkv, j * W + i * cw, H), T.hd[i], k_here, s.sent, pid, rid, m)
+                for sem, there, a, n in ((s.karr, k_here, H, cw - H), (s.varr, v_here, KW, cw)):
+                    g.wait_ge(sem, _count(feed_mask(c, i)))
+                    g.remote_dma(cols(T.fkv, j * W + a + i * cw, n), cols(T.kv, a + i * cw, n), there, s.sent, pid, rid, m)
+                g.wait_ge(s.sent, 3 * _count(m))

from concourse.bass import DstId, RemoteDMATransfer
from concourse.mybir import AluOpType

P = 128
QP = 32
KB = 2
NF = 4
NN = 2
NC = 4
KW = KB * P
W = 2 * KW
H = 8

SCRATCH = {
    "qs": ("sbuf", [P, QP], "bfloat16"),
    "kv": ("sbuf", [P, W], "bfloat16"),
    "hd": ("dram", [NC, P, H], "bfloat16"),
    "fkv": ("sbuf", [P, NF * W], "bfloat16"),
    "nv": ("sbuf", [P, NN * KW], "bfloat16"),
    "ns": ("sbuf", [P, NN * KB * QP], "bfloat16"),
    "zero": ("sbuf", [P, KB * QP], "float32"),
    "ss": ("sbuf", [P, KB * QP], "bfloat16"),
    "sf": ("sbuf", [P, NF * KB * QP], "bfloat16"),
    "ob": ("sbuf", [P, QP], "bfloat16"),
    "ps_s": ("psum", [P, 512], "float32"),
    "ps_o": ("psum", [P, 512], "float32"),
}
for _j in range(NF):
    SCRATCH["ps_f%d" % _j] = ("psum", [P, 512], "float32")
SEMAPHORES = ["qld", "kld", "vld", "hld", "qarr", "harr", "karr", "varr", "narr", "nvarr", "sent",
              "zr", "m1", "rl", "m2", "yr", "st"]
SEMAPHORES += [n % j for j in range(NF) for n in ("ka%d", "mf%d", "rf%d")]
SEMAPHORES += ["vb%d" % i for i in range(NF * KB)]


def _bits(mask):
    return [b for b in range(mask.bit_length()) if (mask >> b) & 1]


def _part(mask, i, n):
    b = _bits(mask)
    w = len(b) // n
    return sum(1 << e for e in b[i * w:(i + 1) * w])


def _count(mask):
    return len(_bits(mask))


def _plan(T, topo):
    cores = list(T.cores)
    root = cores[T.root]
    every = range(topo.CORES_PER_CHIP * topo.CHIPS)
    near = [c for c in cores if c != root and topo.may_write(root, c) and topo.may_write(c, root)]
    far = [c for c in cores if c != root and c not in near]

    def owners(c):
        free = [x for x in every if topo.chip(x) == topo.chip(c) and x not in cores and topo.may_write(x, root)]
        dies = sorted({topo.die(x) for x in free}, key=lambda d: d != topo.die(c))
        first = [[x for x in free if topo.die(x) == d] for d in dies]
        return [first[b % len(first)][b // len(first)] for b in range(len(free))][0:NC]

    carriers = {c: owners(c) for c in far}
    beside = [c for c in far if topo.mates(topo.chip(c), topo.chip(root))]
    beyond = [c for c in far if c not in beside and all(topo.may_write(c, x) for b in beside for x in owners(b))]
    if beside and beyond:
        pool = owners(beside[0])
        carriers[beside[0]], carriers[beyond[0]] = pool[0:len(pool) // 2], pool[len(pool) // 2:]
    return root, near, far, carriers


def _send(topo, dst, mask, sem, src, out):
    rid, pid, _ = topo.addr(dst)
    return RemoteDMATransfer(dst_ids=[DstId(rid=rid, pnc=pid)], dma_engine_mask=mask, remote_sem=sem, src=src, dst=out)


def _scores(g, T, need):
    s = T.sem
    g.vector.memset(T.zero[:], 0.0).then_inc(s.zr, 1)
    for sem, n in need:
        g.tensor.wait_ge(sem, n)
    for b in range(KB):
        g.tensor.matmul(T.ps_s[:, b * QP:(b + 1) * QP], T.kv[:, b * P:(b + 1) * P], T.qs[:],
                        start=True, stop=True).then_inc(s.m1, 1)
    g.vector.wait_ge(s.zr, 1)
    g.vector.wait_ge(s.m1, KB)
    g.vector.tensor_tensor(T.ss[:], T.ps_s[:, 0:KB * QP], T.zero[:], AluOpType.max).then_inc(s.rl, 1)


def rank_program(g, core, T, topo):
    s = T.sem
    root, near, far, carriers = _plan(T, topo)
    kcols, vcols = T.kv[:, 0:KW], T.kv[:, KW:W]
    nf, nn = len(far), len(near)

    def cols(t, a, n):
        return t[:, a:a + n]

    def q_mask(c):
        return _part(topo.mask(root, c), near.index(c), nn)

    def head_mask(c, i):
        m = topo.mask(c, carriers[c][i])
        return _part(m, i, _count(m))

    def feed_mask(c, i):
        return _part(topo.mask(c, carriers[c][i]), i, len(carriers[c]))

    def c_mask(x):
        return topo.mask(x, root)

    if core == root:
        g.sync.dma_start(T.qs[:], T.q[:]).then_inc(s.qld, 16)
        g.scalar.wait_ge(s.qld, 16)
        g.scalar.dma_start(kcols, T.k[:]).then_inc(s.kld, 16)
        g.scalar.dma_start(vcols, T.v[:]).then_inc(s.vld, 16)
        g.wait_ge(s.qld, 16)
        g.remote_dma_fused([_send(topo, c, q_mask(c), s.qarr, T.qs[:], T.qs[:]) for c in near], local_sem=s.sent)
        _scores(g, T, [(s.qld, 16), (s.kld, 16)])
        g.tensor.wait_ge(s.rl, 1)
        g.tensor.wait_ge(s.vld, 16)
        for b in range(KB):
            g.tensor.matmul(T.ps_o[:, 0:QP], cols(T.kv, KW + b * P, P), cols(T.ss, b * QP, QP),
                            start=(b == 0), stop=False).then_inc(s.m2, 1)
        back = sum(_count(topo.mask(c, root)) for c in near)
        g.tensor.wait_ge(s.nvarr, back)
        g.tensor.wait_ge(s.narr, back)
        for i in range(nn * KB):
            g.tensor.matmul(T.ps_o[:, 0:QP], cols(T.nv, i * P, P), cols(T.ns, i * QP, QP),
                            start=False, stop=False).then_inc(s.m2, 1)
        order = sorted(range(nf), key=lambda j: (topo.chip(carriers[far[j]][0]) != topo.chip(far[j]),
                                                 -len(carriers[far[j]])))
        for j in order:
            g.tensor.wait_ge(s["ka%d" % j], 2 * sum(_count(c_mask(x)) for x in carriers[far[j]]))
            pf = T["ps_f%d" % j]
            for b in range(KB):
                g.tensor.matmul(cols(pf, b * QP, QP), cols(T.fkv, j * W + b * P, P), T.qs[:],
                                start=True, stop=True).then_inc(s["mf%d" % j], 1)
            g.vector.wait_ge(s["mf%d" % j], KB)
            g.vector.tensor_tensor(cols(T.sf, j * KB * QP, KB * QP), pf[:, 0:KB * QP], T.zero[:],
                                   AluOpType.max).then_inc(s["rf%d" % j], 1)
        for j in order:
            g.tensor.wait_ge(s["rf%d" % j], 1)
            per = len(carriers[far[j]]) // KB
            for b in range(KB):
                g.tensor.wait_ge(s["vb%d" % (j * KB + b)],
                                 sum(_count(c_mask(x)) for x in carriers[far[j]][b * per:(b + 1) * per]))
                g.tensor.matmul(T.ps_o[:, 0:QP], cols(T.fkv, j * W + KW + b * P, P), cols(T.sf, (j * KB + b) * QP, QP),
                                start=False, stop=(j == order[-1] and b == KB - 1)).then_inc(s.m2, 1)
        g.vector.wait_ge(s.m2, (1 + nn + nf) * KB)
        g.vector.tensor_copy(T.ob[:], T.ps_o[:, 0:QP]).then_inc(s.yr, 1)
        g.sync.wait_ge(s.yr, 1)
        g.sync.dma_start(T.y[:], T.ob[:]).then_inc(s.st, 16)
        g.wait_ge(s.sent, sum(_count(q_mask(c)) for c in near))
        g.wait_ge(s.st, 16)

    elif core in near:
        i = near.index(core)
        rid, pid, _ = topo.addr(root)
        m = topo.mask(core, root)
        g.sync.dma_start(vcols, T.v[:]).then_inc(s.vld, 16)
        g.scalar.dma_start(kcols, T.k[:]).then_inc(s.kld, 16)
        g.wait_ge(s.vld, 16)
        g.remote_dma(cols(T.nv, i * KW, KW), vcols, s.nvarr, s.sent, pid, rid, m)
        _scores(g, T, [(s.kld, 16), (s.qarr, _count(q_mask(core)))])
        g.wait_ge(s.rl, 1)
        g.remote_dma(cols(T.ns, i * KB * QP, KB * QP), T.ss[:], s.narr, s.sent, pid, rid, m)
        g.wait_ge(s.sent, 2 * _count(m))

    elif core in far:
        mine = carriers[core]
        nc = len(mine)
        cw = KW // nc
        for i in range(nc):
            (g.sync, g.scalar)[i % 2].dma_start(T.hd[i], cols(T.k, i * cw, H)).then_inc(s.hld, 16)
        g.sync.dma_start(kcols, T.k[:]).then_inc(s.kld, 16)
        g.scalar.dma_start(vcols, T.v[:]).then_inc(s.vld, 16)
        g.wait_ge(s.hld, 16 * nc)
        g.remote_dma_fused([_send(topo, mine[i], head_mask(core, i), s.harr, T.hd[i], T.hd[i]) for i in range(nc)],
                           local_sem=s.sent)
        for loaded, sem, a, n in ((s.kld, s.karr, H, cw - H), (s.vld, s.varr, KW, cw)):
            g.wait_ge(loaded, 16)
            g.remote_dma_fused([_send(topo, mine[i], feed_mask(core, i), sem,
                                      cols(T.kv, a + i * cw, n), cols(T.kv, a + i * cw, n)) for i in range(nc)],
                               local_sem=s.sent)
        g.wait_ge(s.sent, sum(_count(head_mask(core, i)) + 2 * _count(feed_mask(core, i)) for i in range(nc)))

    else:
        for j, c in enumerate(far):
            if core in carriers[c]:
                i = carriers[c].index(core)
                cw = KW // len(carriers[c])
                rid, pid, _ = topo.addr(root)
                m = c_mask(core)
                k_here, v_here = s["ka%d" % j], s["vb%d" % (j * KB + i * cw // P)]
                g.wait_ge(s.harr, _count(head_mask(c, i)))
                g.remote_dma(cols(T.fkv, j * W + i * cw, H), T.hd[i], k_here, s.sent, pid, rid, m)
                for sem, there, a, n in ((s.karr, k_here, H, cw - H), (s.varr, v_here, KW, cw)):
                    g.wait_ge(sem, _count(feed_mask(c, i)))
                    g.remote_dma(cols(T.fkv, j * W + a + i * cw, n), cols(T.kv, a + i * cw, n), there, s.sent, pid, rid, m)
                g.wait_ge(s.sent, 3 * _count(m))
